import numpy as np
import ml_dtypes


def mxq(x, axis, fmt="e4m3"):
    dtype, down = {"e4m3": (ml_dtypes.float8_e4m3fn, 7), "e5m2": (ml_dtypes.float8_e5m2, 14)}[fmt]
    v = np.moveaxis(np.asarray(x, np.float32).astype(ml_dtypes.bfloat16).astype(np.float64), axis, -1)
    blocks = v.reshape(v.shape[:-1] + (-1, 32))
    amax = np.abs(blocks).max(-1, keepdims=True)
    byte = np.maximum(np.where(amax > 0, np.frexp(amax)[1] - 1 + 127, 0) - down, 1)
    scale = np.exp2(byte - 127.0)
    codes = (blocks / scale).astype(np.float32).astype(dtype).astype(np.float64)
    return np.moveaxis((codes * scale).reshape(v.shape), -1, axis)


WIDE = False


def mx_kscale(k):
    if not WIDE:
        return np.ones(k)
    levels = np.array([10, -10, 5, -5, 0])
    if k % 512:
        return np.exp2(np.random.permutation(np.resize(levels, k // 32))).repeat(32)
    a = np.empty((k // 512, 16))
    for p in range(k // 512):
        a[p, :8] = np.random.permutation(np.resize(levels, 8))
        for g in range(8):
            far = levels[np.abs(levels - a[p, g]) >= 10]
            a[p, g + 8] = far[np.random.randint(len(far))]
    return np.exp2(a.ravel()).repeat(32)


def f64(x):
    return np.asarray(x).astype(np.float64)


def striped(idx):
    return np.tile(idx.reshape(-1, 16).T, (8, 1)).astype(np.uint16)


def unstriped(offs):
    return offs[:16].T.reshape(-1).astype(np.int64)


def striped8(idx):
    return np.concatenate([x.reshape(-1, 16).T for x in idx]).astype(np.uint16)


def runs(offs, k):
    lists = np.stack([offs[16 * r : 16 * r + 16].T.reshape(-1) for r in range(8)]).astype(np.int64)
    return lists[np.arange(k) % 512 // 64]


def pack_weight(w):
    k, n = w.shape
    w = f64(np.asarray(w, np.float32).astype(ml_dtypes.bfloat16)).reshape(k // 32, 32, n)
    amax = np.abs(w).max(1)
    byte = np.clip(np.where(amax > 0, np.frexp(amax)[1] - 1 + 127 - 7, 1), 1, 254)
    scaled = (w * np.exp2(127.0 - byte)[:, None, :]).reshape(k, n).astype(np.float32)
    words = np.ascontiguousarray(scaled.reshape(k // 512, 128, 4, n).transpose(0, 1, 3, 2)).astype(ml_dtypes.float8_e4m3fn).view(np.uint8)
    return words, np.ascontiguousarray(byte.astype(np.uint8).reshape(k // 512, 16, n))


def unpack_weight(words, scales):
    g, p, n, _ = words.shape
    vals = np.ascontiguousarray(words).view(ml_dtypes.float8_e4m3fn).astype(np.float64) * np.repeat(np.exp2(scales.astype(np.float64) - 127.0), 8, axis=1)[..., None]
    return vals.transpose(0, 1, 3, 2).reshape(g * 512, n)


E2M1 = np.array([0.0, 0.5, 1.0, 1.5, 2.0, 3.0, 4.0, 6.0, -0.0, -0.5, -1.0, -1.5, -2.0, -3.0, -4.0, -6.0])


def pack_fp4(w):
    k, n = w.shape
    w = f64(np.asarray(w, np.float32).astype(ml_dtypes.bfloat16)).reshape(k // 32, 32, n)
    amax = np.abs(w).max(1)
    mant, ex = np.frexp(amax / 6.0)
    byte = np.clip(np.where(amax > 0, np.where(mant > 0.5, ex, ex - 1) + 127, 1), 1, 254)
    scaled = (w * np.exp2(127.0 - byte)[:, None, :]).reshape(k, n).astype(np.float32)
    c = np.ascontiguousarray(scaled.reshape(k // 512, 128, 4, n).transpose(0, 1, 3, 2)).astype(ml_dtypes.float4_e2m1fn).view(np.uint8) & 0xF
    words = (c[..., 0::2] | (c[..., 1::2] << 4)).reshape(k // 512, 128, 2 * n)
    return np.ascontiguousarray(words), np.ascontiguousarray(byte.astype(np.uint8).reshape(k // 512, 16, n))


def unpack_fp4(words, scales):
    g, _, n = scales.shape
    words = np.ascontiguousarray(words).reshape(g, 128, n, 2)
    nib = np.empty((g, 128, n, 4), np.uint8)
    nib[..., 0::2] = words & 0xF
    nib[..., 1::2] = words >> 4
    vals = E2M1[nib] * np.repeat(np.exp2(scales.astype(np.float64) - 127.0), 8, axis=1)[..., None]
    return vals.transpose(0, 1, 3, 2).reshape(g * 512, n)


def planes(y):
    n, m = y.shape
    v = y.astype(np.float32).astype(ml_dtypes.bfloat16).astype(np.float64).reshape(n // 32, 32, m)
    top = np.abs(v).max(1)
    byte = np.clip(np.where(top > 0, np.frexp(top)[1] - 1 + 127 - 7, 1), 1, 254)
    codes = (v * np.exp2(127.0 - byte)[:, None, :]).reshape(n, m).astype(np.float32).astype(ml_dtypes.float8_e4m3fn).view(np.uint8)
    words = codes.reshape(n // 512, 128, 4, m).transpose(0, 1, 3, 2)
    return np.ascontiguousarray(words), np.ascontiguousarray(byte.astype(np.uint8).reshape(n // 512, 16, m))


K, T, S, N, H = 512, 2048, 512, 512, 512


def setup_inputs():
    n = np.random.standard_normal
    s = mx_kscale(K)[:, None]
    u = mx_kscale(H)
    packed_xT = pack_weight(n((K, T)) * s)
    packed_w1 = pack_fp4(n((K, H)) / np.sqrt(K) / s)
    packed_w2 = pack_fp4(n((H, N)) / np.sqrt(H) / u[:, None])
    return {
        "x_words": packed_xT[0],
        "x_scales": packed_xT[1],
        "w1_words": packed_w1[0],
        "w1_scales": packed_w1[1],
        "gn": (np.random.uniform(0.5, 1.5, (H, 1)) * u[:, None]).astype(np.float32),
        "w2_words": packed_w2[0],
        "w2_scales": packed_w2[1],
        "offs": striped(np.random.permutation(T)[:S]),
        "n1": striped8(np.stack([np.random.permutation(S) for _ in range(8)])),
        "n2": striped8(np.stack([np.random.permutation(S) for _ in range(8)])),
        "n3": striped8(np.stack([np.random.permutation(S) for _ in range(8)])),
        "n4": striped8(np.stack([np.random.permutation(S) for _ in range(8)])),
        "n5": striped8(np.stack([np.random.permutation(S) for _ in range(8)])),
    }


def reference(x_words, x_scales, w1_words, w1_scales, gn, w2_words, w2_scales, offs, n1, n2, n3, n4, n5):
    xq = unpack_weight(x_words, x_scales)[:, unstriped(offs)]
    y = unpack_fp4(w1_words, w1_scales).T @ xq
    st = y - (y[np.arange(H)[:, None], runs(n1, H)])
    su = np.maximum(st, st[np.arange(H)[:, None], runs(n2, H)])
    z = f64(gn) * (su + 0.5 * (su[np.arange(H)[:, None], runs(n3, H)]))
    h = unpack_fp4(w2_words, w2_scales).T @ mxq(z, 0, "e4m3")
    out_0 = (h * (h[np.arange(N)[:, None], runs(n4, N)])) * (np.tanh(h[np.arange(N)[:, None], runs(n5, N)]))
    return (out_0,) + planes(out_0)

@@ -1,0 +1,237 @@
+from contextlib import ExitStack
+
+import concourse.mybir as mybir
+
+K, T, S, N, H = 512, 2048, 512, 512, 512
+P = 128
+PACK = 4
+FLOPS = 2 * K * H * S + 2 * H * N * S
+
+F32 = mybir.dt.float32
+BF16 = mybir.dt.bfloat16
+I32 = mybir.dt.int32
+U32 = mybir.dt.uint32
+U16 = mybir.dt.uint16
+U8 = mybir.dt.uint8
+FP8X4 = mybir.dt.float8_e4m3fn_x4
+FP4X4 = mybir.dt.float4_e2m1fn_x4
+ALU = mybir.AluOpType
+ACT = mybir.ActivationFunctionType
+
+Z_CHUNKS = [256,128,128]
+O_CHUNKS = [256,128,128]
+
+
+def spans(widths):
+    out, at = [], 0
+    for w in widths:
+        out.append((at, at + w))
+        at = at + w
+    return out
+
+
+def interleave(copy, grouped, planes):
+    copy(grouped.rearrange("p (c i t) -> p c t i", i=4, t=PACK), planes.rearrange("p t (c i) -> p c t i", i=4))
+
+
+def tile_picked_laythreecube_none_po_kernel(
+    tc, x_words, x_scales, w1_words, w1_scales, gn, w2_words, w2_scales, offs, n1, n2, n3, n4, n5, out_0, out_1, out_2
+):
+    nc = tc.nc
+    with ExitStack() as ctx:
+        keep = ctx.enter_context(tc.tile_pool(name="keep", bufs=1))
+        psum = ctx.enter_context(tc.psum_pool(name="psum", bufs=1))
+
+        def sb(name, shape, dtype, tag=None):
+            return keep.tile(shape, dtype, name=name, tag=tag or name, align_bytes=64)
+
+        lists = {name: sb("list_" + name, [P, S // 16], U16) for name in ("offs", "n1", "n2", "n3", "n4", "n5")}
+        x_w = sb("x_w", [P, T], U32)
+        x_s = sb("x_s", [P, T], U8)
+        w_raw = [sb("w_raw%d" % l, [P, 2 * H], U8) for l in range(2)]
+        ws_raw = [sb("ws_raw%d" % l, [P, H], U8) for l in range(2)]
+        gain = sb("gain", [P, PACK], F32)
+        half_gain = sb("half_gain", [P, PACK], F32)
+
+        nc.gpsimd.memset(ws_raw[0][:].bitcast(I32), 0)
+        nc.vector.memset(x_s[:, : T // 2].bitcast(I32), 0)
+        nc.gpsimd.memset(x_s[:, T // 2 :].bitcast(I32), 0)
+
+        def load_scales(queues, tile_cols, rows):
+            for q in range(4):
+                queues[q].dma_start(
+                    tile_cols[32 * q : 32 * q + 4, :].bitcast(I32), rows[0, 4 * q : 4 * q + 4, :].bitcast(I32)
+                )
+
+        nc.sync.dma_start(lists["offs"][:], offs)
+        nc.scalar.dma_start(w_raw[0][:].bitcast(I32), w1_words[0].bitcast(I32))
+        nc.scalar.dma_start(x_w[:].bitcast(I32), x_words[0].rearrange("p n t -> p (n t)").bitcast(I32))
+        load_scales([nc.sync] * 2 + [nc.gpsimd] * 2, ws_raw[0], w1_scales)
+        load_scales([nc.sync] * 4, x_s, x_scales)
+        nc.gpsimd.memset(ws_raw[1][:].bitcast(I32), 0)
+        nc.sync.dma_start(lists["n1"][:], n1)
+        nc.sync.dma_start(w_raw[1][:].bitcast(I32), w2_words[0].bitcast(I32))
+        load_scales([nc.sync] * 4, ws_raw[1], w2_scales)
+        nc.sync.dma_start(lists["n2"][:], n2)
+        nc.sync.dma_start(gain[:], gn.rearrange("(p t) o -> p (t o)", t=PACK))
+        nc.sync.dma_start(lists["n3"][:], n3)
+        nc.sync.dma_start(lists["n5"][:], n5)
+        nc.sync.dma_start(lists["n4"][:], n4)
+
+        wide_a = [sb("wide_a%d" % t, [P, 2 * S], F32) for t in range(PACK)]
+        wide_b = [sb("wide_b%d" % t, [P, 2 * S], F32) for t in range(PACK)]
+        wide_c = [sb("wide_c%d" % t, [P, 2 * S], F32, tag="late" if t == PACK - 1 else None) for t in range(PACK)]
+        for t in range(PACK):
+            nc.vector.memset(wide_a[t][:, S:].bitcast(I32), 0)
+        y = [wide_b[(t - 1) % PACK][:, S:] for t in range(PACK)]
+
+        w_dealt = [sb("w_dealt%d" % l, [P, 2 * H], U8) for l in range(2)]
+        ws_dealt = [sb("ws_dealt%d" % l, [P, H], U8) for l in range(2)]
+
+        def deal(l):
+            nc.vector.tensor_copy(
+                w_dealt[l][:].rearrange("p (t m b) -> p t m b", t=PACK, b=2),
+                w_raw[l][:].rearrange("p (m t b) -> p t m b", t=PACK, b=2),
+            )
+            nc.vector.tensor_copy(
+                ws_dealt[l][:].rearrange("p (t m) -> p t m", t=PACK),
+                ws_raw[l][:].rearrange("p (m t) -> p t m", t=PACK),
+            )
+
+        def product(l, t, bank, codes, scales):
+            nc.tensor.matmul_mx(
+                bank,
+                lhsT=w_dealt[l][:, 2 * P * t : 2 * P * (t + 1)].bitcast(FP4X4),
+                lhsT_scale=ws_dealt[l][:, P * t : P * (t + 1)],
+                rhs=codes.bitcast(FP8X4),
+                rhs_scale=scales,
+                start=True,
+                stop=True,
+            )
+
+        picked_w = sb("picked_w", [P, S], U32)
+        picked_s = sb("picked_s", [P, S], U8)
+        deal(0)
+        nc.vector.tensor_copy(picked_s[:], x_s[:].indirect(lists["offs"][:]))
+        nc.vector.tensor_copy(picked_w[:], x_w[:].indirect(lists["offs"][:]))
+        deal(1)
+        nc.scalar.mul(half_gain[:], gain[:], 0.5)
+
+        for t in range(PACK):
+            bank = psum.tile([P, S], F32, name="bank%d" % t)
+            product(0, t, bank[:], picked_w[:], picked_s[:])
+            nc.scalar.mul(wide_a[t][:, :S], bank[:], -1.0)
+            nc.scalar.copy(y[t], bank[:])
+
+        other = [sb("other%d" % t, [P, S], F32) for t in range(PACK)]
+        st2 = [sb("st2_%d" % t, [P, S], F32) for t in range(PACK)]
+        su_late = [sb("su%d" % t, [P, S], F32) for t in range(PACK - 2, PACK)]
+        su = [wide_a[t + 2][:, :S] for t in range(PACK - 2)] + [tile[:] for tile in su_late]
+        gsu = [wide_c[t][:, S:] for t in range(PACK)]
+        hsu = [sb("hsu%d" % t, [P, S], F32) for t in range(PACK)]
+        z_spans = spans(Z_CHUNKS)
+        z_planes = {}
+
+        def step1(t):
+            nc.vector.tensor_tensor(wide_b[t][:, :S], wide_a[t][:].indirect(lists["n1"][:]), y[t], ALU.add)
+
+        def step2(t):
+            nc.vector.tensor_copy(st2[t][:], wide_b[t][:].indirect(lists["n2"][:]))
+
+        def step3(t):
+            nc.vector.tensor_tensor(su[t], wide_b[t][:, :S], st2[t][:], ALU.max)
+            nc.scalar.activation(hsu[t][:], su[t], ACT.Copy, scale=half_gain[:, t : t + 1])
+            nc.scalar.activation(gsu[t], su[t], ACT.Copy, scale=gain[:, t : t + 1])
+
+        def step4(c, t):
+            a, b = z_spans[c]
+            if c not in z_planes:
+                z_planes[c] = sb("z_planes%d" % c, [P, PACK, b - a], F32, tag="su%d" % (c + 1) if c else None)
+            nc.vector.tensor_tensor(
+                z_planes[c][:, t, :], hsu[t][:].indirect(lists["n3"][:, a // 16 : b // 16]), gsu[t][:, a:b], ALU.add
+            )
+
+        step1(0)
+        step1(1)
+        step2(0)
+        step1(2)
+        step3(0)
+        step2(1)
+        step1(3)
+        step3(1)
+        step2(2)
+        step4(0, 0)
+        step3(2)
+        step2(3)
+        step4(0, 1)
+        step3(3)
+        step4(0, 2)
+        for t in range(PACK - 1):
+            step4(1, t)
+        step4(0, 3)
+        step4(1, 3)
+        for t in range(PACK):
+            step4(2, t)
+
+        h = [sb("h%d" % t, [P, S], F32) for t in range(PACK)]
+
+        def z_product(c):
+            a, b = z_spans[c]
+            w = b - a
+            last = c == len(z_spans) - 1
+            grouped = sb("z_grouped%d" % c, [P, PACK * w], BF16)
+            interleave(nc.vector.tensor_copy if last else nc.scalar.copy, grouped[:], z_planes[c][:])
+            codes = sb("z_codes%d" % c, [P, w], U32)
+            scales = sb("z_scales%d" % c, [P, w], U8)
+            nc.vector.quantize_mx(codes[:].bitcast(FP8X4), scales[:], grouped[:])
+            first = psum.tile([P, S], F32, name="first%d" % c)
+            product(1, 0, first[:, :w], codes[:], scales[:])
+            nc.scalar.activation(wide_c[0][:, a:b], first[:, :w], ACT.Tanh)
+            nc.scalar.copy(h[0][:, a:b], first[:, :w])
+            for t in range(1, PACK):
+                product(1, t, h_banks[t][:, a:b], codes[:], scales[:])
+
+        h_banks = {t: psum.tile([P, S], F32, name="bank%d" % t) for t in range(1, PACK)}
+        for c in range(len(z_spans)):
+            z_product(c)
+
+        for t in range(1, PACK):
+            nc.scalar.activation(wide_c[t][:, :S], h_banks[t][:], ACT.Tanh)
+            nc.scalar.copy(h[t][:], h_banks[t][:])
+
+        for t in range(PACK):
+            nc.vector.tensor_tensor(other[t][:], wide_c[t][:].indirect(lists["n5"][:]), h[t][:], ALU.mult)
+
+        o_spans = spans(O_CHUNKS)
+        o_all = sb("o_all", [P, PACK * S], F32, tag="late")
+        o_planes = [o_all[:, PACK * a : PACK * b].rearrange("p (t c) -> p t c", t=PACK) for a, b in o_spans]
+        o_scales = sb("o_scales", [P, S], U8)
+        out_rows = out_0.rearrange("(p t) j -> p t j", t=PACK)
+        out_words = out_1[0].rearrange("p n t -> p (n t)").bitcast(I32)
+
+        def o_gather(c):
+            a, b = o_spans[c]
+            for t in range(PACK):
+                nc.vector.tensor_tensor(
+                    o_planes[c][:, t, :], h[t][:].indirect(lists["n4"][:, a // 16 : b // 16]), other[t][:, a:b], ALU.mult
+                )
+            nc.sync.dma_start(out_rows[:, :, a:b], o_planes[c])
+
+        def o_quantize(c):
+            a, b = o_spans[c]
+            w = b - a
+            last = c == len(o_spans) - 1
+            grouped = sb("o_grouped%d" % c, [P, PACK * w], BF16)
+            interleave(nc.vector.tensor_copy if last else nc.scalar.copy, grouped[:], o_planes[c])
+            codes = sb("o_codes%d" % c, [P, w], U32)
+            nc.vector.quantize_mx(codes[:].bitcast(FP8X4), o_scales[:, a:b], grouped[:])
+            nc.sync.dma_start(out_words[:, a:b], codes[:].bitcast(I32))
+
+        o_gather(0)
+        for c in range(1, len(o_spans)):
+            o_gather(c)
+            o_quantize(c - 1)
+        o_quantize(len(o_spans) - 1)
+        for q in range(4):
+            queue = nc.scalar if q % 2 == 0 else nc.sync
+            queue.dma_start(out_2[0, 4 * q : 4 * q + 4, :].bitcast(I32), o_scales[32 * q : 32 * q + 4, :].bitcast(I32))

@@ -5,6 +5,9 @@ import concourse.mybir as mybir
 K, T, S, N, H = 512, 2048, 512, 512, 512
 P = 128
 PACK = 4
+QUADRANTS = 4
+LIST_ROWS = 16
+HALF = S // 2
 FLOPS = 2 * K * H * S + 2 * H * N * S
 
 F32 = mybir.dt.float32
@@ -18,16 +21,8 @@ FP4X4 = mybir.dt.float4_e2m1fn_x4
 ALU = mybir.AluOpType
 ACT = mybir.ActivationFunctionType
 
-Z_CHUNKS = [256,128,128]
-O_CHUNKS = [256,128,128]
-
-
-def spans(widths):
-    out, at = [], 0
-    for w in widths:
-        out.append((at, at + w))
-        at = at + w
-    return out
+CHUNKS = ((0, 256), (256, 384), (384, 512))
+LAST = len(CHUNKS) - 1
 
 
 def interleave(copy, grouped, planes):
@@ -45,193 +40,208 @@ def tile_picked_laythreecube_none_po_kernel(
         def sb(name, shape, dtype, tag=None):
             return keep.tile(shape, dtype, name=name, tag=tag or name, align_bytes=64)
 
-        lists = {name: sb("list_" + name, [P, S // 16], U16) for name in ("offs", "n1", "n2", "n3", "n4", "n5")}
+        lists = {name: sb("list_" + name, [P, S // LIST_ROWS], U16) for name in ("offs", "n1", "n2", "n3", "n4", "n5")}
+
+        def entries(name, a, b):
+            return lists[name][:, a // LIST_ROWS : b // LIST_ROWS]
+
         x_w = sb("x_w", [P, T], U32)
         x_s = sb("x_s", [P, T], U8)
-        w_raw = [sb("w_raw%d" % l, [P, 2 * H], U8) for l in range(2)]
-        ws_raw = [sb("ws_raw%d" % l, [P, H], U8) for l in range(2)]
+        w_raw = [sb("w_raw%d" % layer, [P, 2 * H], U8) for layer in range(2)]
+        ws_raw = [sb("ws_raw%d" % layer, [P, H], U8) for layer in range(2)]
         gain = sb("gain", [P, PACK], F32)
         half_gain = sb("half_gain", [P, PACK], F32)
 
-        nc.gpsimd.memset(ws_raw[0][:].bitcast(I32), 0)
         nc.vector.memset(x_s[:, : T // 2].bitcast(I32), 0)
         nc.gpsimd.memset(x_s[:, T // 2 :].bitcast(I32), 0)
+        nc.gpsimd.memset(ws_raw[0][:].bitcast(I32), 0)
 
-        def load_scales(queues, tile_cols, rows):
-            for q in range(4):
+        def load_scales(queues, tile, rows):
+            for q in range(QUADRANTS):
                 queues[q].dma_start(
-                    tile_cols[32 * q : 32 * q + 4, :].bitcast(I32), rows[0, 4 * q : 4 * q + 4, :].bitcast(I32)
+                    tile[32 * q : 32 * q + PACK, :].bitcast(I32), rows[0, PACK * q : PACK * (q + 1), :].bitcast(I32)
                 )
 
         nc.sync.dma_start(lists["offs"][:], offs)
         nc.scalar.dma_start(w_raw[0][:].bitcast(I32), w1_words[0].bitcast(I32))
         nc.scalar.dma_start(x_w[:].bitcast(I32), x_words[0].rearrange("p n t -> p (n t)").bitcast(I32))
-        load_scales([nc.sync] * 2 + [nc.gpsimd] * 2, ws_raw[0], w1_scales)
-        load_scales([nc.sync] * 4, x_s, x_scales)
-        nc.gpsimd.memset(ws_raw[1][:].bitcast(I32), 0)
+        load_scales([nc.sync] * QUADRANTS, x_s, x_scales)
+        load_scales([nc.sync] * (QUADRANTS - 1) + [nc.gpsimd], ws_raw[0], w1_scales)
+        nc.gpsimd.dma_start(gain[:], gn.rearrange("(p t) o -> p (t o)", t=PACK))
+
+        win1 = [sb("win1_%d" % t, [P, 2 * S], F32) for t in range(PACK)]
+        win2 = [sb("win2_%d" % t, [P, 2 * S], F32) for t in range(PACK)]
+        win5 = [
+            sb("win5_%d" % t, [P, 2 * S], F32, tag="out_planes" if t == PACK - 2 else None) for t in range(PACK)
+        ]
+        nc.vector.memset(win1[0][:, S:], 0.0)
+        nc.vector.memset(ws_raw[1][:].bitcast(I32), 0)
+        for t in range(1, PACK):
+            nc.scalar.copy(win1[t][:, S:], win1[0][:, S:])
+        y = [win2[(t - 1) % PACK][:, S:] for t in range(PACK)]
+
         nc.sync.dma_start(lists["n1"][:], n1)
         nc.sync.dma_start(w_raw[1][:].bitcast(I32), w2_words[0].bitcast(I32))
-        load_scales([nc.sync] * 4, ws_raw[1], w2_scales)
+        load_scales([nc.sync] * QUADRANTS, ws_raw[1], w2_scales)
         nc.sync.dma_start(lists["n2"][:], n2)
-        nc.sync.dma_start(gain[:], gn.rearrange("(p t) o -> p (t o)", t=PACK))
         nc.sync.dma_start(lists["n3"][:], n3)
         nc.sync.dma_start(lists["n5"][:], n5)
         nc.sync.dma_start(lists["n4"][:], n4)
 
-        wide_a = [sb("wide_a%d" % t, [P, 2 * S], F32) for t in range(PACK)]
-        wide_b = [sb("wide_b%d" % t, [P, 2 * S], F32) for t in range(PACK)]
-        wide_c = [sb("wide_c%d" % t, [P, 2 * S], F32, tag="late" if t == PACK - 1 else None) for t in range(PACK)]
-        for t in range(PACK):
-            nc.vector.memset(wide_a[t][:, S:].bitcast(I32), 0)
-        y = [wide_b[(t - 1) % PACK][:, S:] for t in range(PACK)]
+        w_dealt = {}
+        ws_dealt = {}
 
-        w_dealt = [sb("w_dealt%d" % l, [P, 2 * H], U8) for l in range(2)]
-        ws_dealt = [sb("ws_dealt%d" % l, [P, H], U8) for l in range(2)]
-
-        def deal(l):
+        def deal_words(layer, tag=None):
+            w_dealt[layer] = sb("w_dealt%d" % layer, [P, 2 * H], U8, tag=tag)
             nc.vector.tensor_copy(
-                w_dealt[l][:].rearrange("p (t m b) -> p t m b", t=PACK, b=2),
-                w_raw[l][:].rearrange("p (m t b) -> p t m b", t=PACK, b=2),
-            )
-            nc.vector.tensor_copy(
-                ws_dealt[l][:].rearrange("p (t m) -> p t m", t=PACK),
-                ws_raw[l][:].rearrange("p (m t) -> p t m", t=PACK),
+                w_dealt[layer][:].rearrange("p (t m b) -> p t m b", t=PACK, b=2),
+                w_raw[layer][:].rearrange("p (m t b) -> p t m b", t=PACK, b=2),
             )
 
-        def product(l, t, bank, codes, scales):
+        def deal_scales(layer):
+            ws_dealt[layer] = sb("ws_dealt%d" % layer, [P, H], U8)
+            nc.vector.tensor_copy(
+                ws_dealt[layer][:].rearrange("p (t m) -> p t m", t=PACK),
+                ws_raw[layer][:].rearrange("p (m t) -> p t m", t=PACK),
+            )
+
+        def product(layer, t, result, codes, scales):
             nc.tensor.matmul_mx(
-                bank,
-                lhsT=w_dealt[l][:, 2 * P * t : 2 * P * (t + 1)].bitcast(FP4X4),
-                lhsT_scale=ws_dealt[l][:, P * t : P * (t + 1)],
+                result,
+                lhsT=w_dealt[layer][:, 2 * P * t : 2 * P * (t + 1)].bitcast(FP4X4),
+                lhsT_scale=ws_dealt[layer][:, P * t : P * (t + 1)],
                 rhs=codes.bitcast(FP8X4),
                 rhs_scale=scales,
                 start=True,
                 stop=True,
             )
 
-        picked_w = sb("picked_w", [P, S], U32)
         picked_s = sb("picked_s", [P, S], U8)
-        deal(0)
+        deal_words(0)
         nc.vector.tensor_copy(picked_s[:], x_s[:].indirect(lists["offs"][:]))
-        nc.vector.tensor_copy(picked_w[:], x_w[:].indirect(lists["offs"][:]))
-        deal(1)
+        picked_lo = sb("picked_lo", [P, HALF], U32)
+        nc.vector.tensor_copy(picked_lo[:], x_w[:].indirect(entries("offs", 0, HALF)))
+        deal_scales(0)
+        picked_hi = sb("picked_hi", [P, HALF], U32, tag="ws_raw0")
+        nc.vector.tensor_copy(picked_hi[:], x_w[:].indirect(entries("offs", HALF, S)))
+        deal_words(1, tag="x_w")
+        deal_scales(1)
         nc.scalar.mul(half_gain[:], gain[:], 0.5)
+        picked = ((picked_lo, slice(0, HALF)), (picked_hi, slice(HALF, S)))
 
-        for t in range(PACK):
-            bank = psum.tile([P, S], F32, name="bank%d" % t)
-            product(0, t, bank[:], picked_w[:], picked_s[:])
-            nc.scalar.mul(wide_a[t][:, :S], bank[:], -1.0)
+        for u, (words, cols) in enumerate(picked):
+            bank = psum.tile([P, S], F32, name="plane0_%d" % u)
+            product(0, 0, bank[:, :HALF], words[:], picked_s[:, cols])
+            nc.scalar.mul(win1[0][:, cols], bank[:, :HALF], -1.0)
+            nc.scalar.copy(y[0][:, cols], bank[:, :HALF])
+        for t in range(1, PACK):
+            bank = psum.tile([P, S], F32, name="plane%d" % t)
+            for words, cols in reversed(picked):
+                product(0, t, bank[:, cols], words[:], picked_s[:, cols])
+            nc.scalar.mul(win1[t][:, :S], bank[:], -1.0)
             nc.scalar.copy(y[t], bank[:])
 
-        other = [sb("other%d" % t, [P, S], F32) for t in range(PACK)]
-        st2 = [sb("st2_%d" % t, [P, S], F32) for t in range(PACK)]
-        su_late = [sb("su%d" % t, [P, S], F32) for t in range(PACK - 2, PACK)]
-        su = [wide_a[t + 2][:, :S] for t in range(PACK - 2)] + [tile[:] for tile in su_late]
-        gsu = [wide_c[t][:, S:] for t in range(PACK)]
-        hsu = [sb("hsu%d" % t, [P, S], F32) for t in range(PACK)]
-        z_spans = spans(Z_CHUNKS)
-        z_planes = {}
+        h_tanh = [sb("h_tanh%d" % t, [P, S], F32) for t in range(PACK)]
+        st_n2 = [sb("st_n2_%d" % t, [P, S], F32) for t in range(PACK)]
+        su_own = [sb("su%d" % t, [P, S], F32) for t in range(PACK - 2, PACK)]
+        su = [win1[t + 2][:, :S] for t in range(PACK - 2)] + [tile[:] for tile in su_own]
+        gain_su = [win5[t][:, S:] for t in range(PACK)]
+        win3 = [sb("win3_%d" % t, [P, S], F32) for t in range(PACK)]
 
-        def step1(t):
-            nc.vector.tensor_tensor(wide_b[t][:, :S], wide_a[t][:].indirect(lists["n1"][:]), y[t], ALU.add)
-
-        def step2(t):
-            nc.vector.tensor_copy(st2[t][:], wide_b[t][:].indirect(lists["n2"][:]))
-
-        def step3(t):
-            nc.vector.tensor_tensor(su[t], wide_b[t][:, :S], st2[t][:], ALU.max)
-            nc.scalar.activation(hsu[t][:], su[t], ACT.Copy, scale=half_gain[:, t : t + 1])
-            nc.scalar.activation(gsu[t], su[t], ACT.Copy, scale=gain[:, t : t + 1])
-
-        def step4(c, t):
-            a, b = z_spans[c]
-            if c not in z_planes:
-                z_planes[c] = sb("z_planes%d" % c, [P, PACK, b - a], F32, tag="su%d" % (c + 1) if c else None)
-            nc.vector.tensor_tensor(
-                z_planes[c][:, t, :], hsu[t][:].indirect(lists["n3"][:, a // 16 : b // 16]), gsu[t][:, a:b], ALU.add
-            )
-
-        step1(0)
-        step1(1)
-        step2(0)
-        step1(2)
-        step3(0)
-        step2(1)
-        step1(3)
-        step3(1)
-        step2(2)
-        step4(0, 0)
-        step3(2)
-        step2(3)
-        step4(0, 1)
-        step3(3)
-        step4(0, 2)
-        for t in range(PACK - 1):
-            step4(1, t)
-        step4(0, 3)
-        step4(1, 3)
-        for t in range(PACK):
-            step4(2, t)
+        for step in range(PACK + 2):
+            t = step
+            if t < PACK:
+                nc.vector.tensor_tensor(win2[t][:, :S], win1[t][:].indirect(lists["n1"][:]), y[t], ALU.add)
+            t = step - 1
+            if 0 <= t < PACK:
+                nc.vector.tensor_copy(st_n2[t][:], win2[t][:].indirect(lists["n2"][:]))
+            t = step - 2
+            if 0 <= t:
+                nc.vector.tensor_tensor(su[t], win2[t][:, :S], st_n2[t][:], ALU.max)
+                nc.scalar.activation(win3[t][:], su[t], ACT.Copy, scale=half_gain[:, t : t + 1])
+                nc.scalar.activation(gain_su[t], su[t], ACT.Copy, scale=gain[:, t : t + 1])
 
         h = [sb("h%d" % t, [P, S], F32) for t in range(PACK)]
+        z_planes = {}
+        z_tags = ("st_n2_2", "su3", "z_grouped0")
 
-        def z_product(c):
-            a, b = z_spans[c]
-            w = b - a
-            last = c == len(z_spans) - 1
-            grouped = sb("z_grouped%d" % c, [P, PACK * w], BF16)
-            interleave(nc.vector.tensor_copy if last else nc.scalar.copy, grouped[:], z_planes[c][:])
-            codes = sb("z_codes%d" % c, [P, w], U32)
-            scales = sb("z_scales%d" % c, [P, w], U8)
-            nc.vector.quantize_mx(codes[:].bitcast(FP8X4), scales[:], grouped[:])
-            first = psum.tile([P, S], F32, name="first%d" % c)
-            product(1, 0, first[:, :w], codes[:], scales[:])
-            nc.scalar.activation(wide_c[0][:, a:b], first[:, :w], ACT.Tanh)
-            nc.scalar.copy(h[0][:, a:b], first[:, :w])
-            for t in range(1, PACK):
-                product(1, t, h_banks[t][:, a:b], codes[:], scales[:])
-
-        h_banks = {t: psum.tile([P, S], F32, name="bank%d" % t) for t in range(1, PACK)}
-        for c in range(len(z_spans)):
-            z_product(c)
-
-        for t in range(1, PACK):
-            nc.scalar.activation(wide_c[t][:, :S], h_banks[t][:], ACT.Tanh)
-            nc.scalar.copy(h[t][:], h_banks[t][:])
-
-        for t in range(PACK):
-            nc.vector.tensor_tensor(other[t][:], wide_c[t][:].indirect(lists["n5"][:]), h[t][:], ALU.mult)
-
-        o_spans = spans(O_CHUNKS)
-        o_all = sb("o_all", [P, PACK * S], F32, tag="late")
-        o_planes = [o_all[:, PACK * a : PACK * b].rearrange("p (t c) -> p t c", t=PACK) for a, b in o_spans]
-        o_scales = sb("o_scales", [P, S], U8)
-        out_rows = out_0.rearrange("(p t) j -> p t j", t=PACK)
-        out_words = out_1[0].rearrange("p n t -> p (n t)").bitcast(I32)
-
-        def o_gather(c):
-            a, b = o_spans[c]
+        def z_gather(c):
+            a, b = CHUNKS[c]
+            z_planes[c] = sb("z_planes%d" % c, [P, PACK, b - a], F32, tag=z_tags[c])
             for t in range(PACK):
                 nc.vector.tensor_tensor(
-                    o_planes[c][:, t, :], h[t][:].indirect(lists["n4"][:, a // 16 : b // 16]), other[t][:, a:b], ALU.mult
+                    z_planes[c][:, t, :], win3[t][:].indirect(entries("n3", a, b)), gain_su[t][:, a:b], ALU.add
                 )
-            nc.sync.dma_start(out_rows[:, :, a:b], o_planes[c])
 
-        def o_quantize(c):
-            a, b = o_spans[c]
-            w = b - a
-            last = c == len(o_spans) - 1
-            grouped = sb("o_grouped%d" % c, [P, PACK * w], BF16)
-            interleave(nc.vector.tensor_copy if last else nc.scalar.copy, grouped[:], o_planes[c])
-            codes = sb("o_codes%d" % c, [P, w], U32)
-            nc.vector.quantize_mx(codes[:].bitcast(FP8X4), o_scales[:, a:b], grouped[:])
+        def h_out(t, a, b, result):
+            nc.scalar.activation(win5[t][:, a:b], result, ACT.Tanh)
+            nc.scalar.copy(h[t][:, a:b], result)
+
+        def z_product(c):
+            a, b = CHUNKS[c]
+            width = b - a
+            grouped = sb("z_grouped%d" % c, [P, PACK * width], BF16)
+            interleave(nc.vector.tensor_copy if c == LAST else nc.scalar.copy, grouped[:], z_planes[c][:])
+            codes = sb("z_codes%d" % c, [P, width], U32)
+            scales = sb("z_scales%d" % c, [P, width], U8)
+            nc.vector.quantize_mx(codes[:].bitcast(FP8X4), scales[:], grouped[:])
+            bank = psum.tile([P, S], F32, name="plane0_%d" % c)
+            product(1, 0, bank[:, :width], codes[:], scales[:])
+            if c == 0:
+                product(1, PACK - 1, bank[:, width:], codes[:], scales[:])
+                h_out(0, a, b, bank[:, :width])
+                for t in range(1, PACK - 1):
+                    early = psum.tile([P, S], F32, name="early%d" % t)
+                    product(1, t, early[:, :width], codes[:], scales[:])
+                    h_out(t, a, b, early[:, :width])
+                h_out(PACK - 1, a, b, bank[:, width:])
+            else:
+                h_out(0, a, b, bank[:, :width])
+                for t in range(1, PACK):
+                    product(1, t, h_rest[t][:, a:b], codes[:], scales[:])
+
+        h_rest = {t: psum.tile([P, S], F32, name="plane%d" % t) for t in range(1, PACK)}
+        for c in range(len(CHUNKS)):
+            z_gather(c)
+            if c >= 1:
+                z_product(c - 1)
+        z_product(LAST)
+        rest = CHUNKS[1][0]
+        for t in range(1, PACK):
+            h_out(t, rest, S, h_rest[t][:, rest:])
+
+        for a, b in ((0, HALF), (HALF, S)):
+            nc.vector.tensor_tensor(h_tanh[0][:, a:b], win5[0][:].indirect(entries("n5", a, b)), h[0][:, a:b], ALU.mult)
+        for t in range(1, PACK):
+            nc.vector.tensor_tensor(h_tanh[t][:], win5[t][:].indirect(lists["n5"][:]), h[t][:], ALU.mult)
+
+        out_all = sb("out_all", [P, PACK * S], F32, tag="out_planes")
+        out_planes = [out_all[:, PACK * a : PACK * b].rearrange("p (t c) -> p t c", t=PACK) for a, b in CHUNKS]
+        out_scales = sb("out_scales", [P, S], U8)
+        out_rows = out_0.rearrange("(p t) j -> p t j", t=PACK)
+        out_words = out_1[0].rearrange("p n t -> p (n t)").bitcast(I32)
+        out_grouped = [sb("out_grouped%d" % c, [P, PACK * (b - a)], BF16) for c, (a, b) in enumerate(CHUNKS)]
+
+        def out_quantize(c):
+            a, b = CHUNKS[c]
+            codes = sb("out_codes%d" % c, [P, b - a], U32)
+            nc.vector.quantize_mx(codes[:].bitcast(FP8X4), out_scales[:, a:b], out_grouped[c][:])
             nc.sync.dma_start(out_words[:, a:b], codes[:].bitcast(I32))
 
-        o_gather(0)
-        for c in range(1, len(o_spans)):
-            o_gather(c)
-            o_quantize(c - 1)
-        o_quantize(len(o_spans) - 1)
-        for q in range(4):
+        for c, (a, b) in enumerate(CHUNKS):
+            for t in range(PACK):
+                nc.vector.tensor_tensor(
+                    out_planes[c][:, t, :], h[t][:].indirect(entries("n4", a, b)), h_tanh[t][:, a:b], ALU.mult
+                )
+            nc.sync.dma_start(out_rows[:, :, a:b], out_planes[c])
+            if c < LAST:
+                interleave(nc.scalar.copy, out_grouped[c][:], out_planes[c])
+        out_quantize(0)
+        interleave(nc.vector.tensor_copy, out_grouped[LAST][:], out_planes[LAST])
+        for c in range(1, len(CHUNKS)):
+            out_quantize(c)
+        for q in range(QUADRANTS):
             queue = nc.scalar if q % 2 == 0 else nc.sync
-            queue.dma_start(out_2[0, 4 * q : 4 * q + 4, :].bitcast(I32), o_scales[32 * q : 32 * q + 4, :].bitcast(I32))
+            queue.dma_start(
+                out_2[0, PACK * q : PACK * (q + 1), :].bitcast(I32), out_scales[32 * q : 32 * q + PACK, :].bitcast(I32)
+            )

@@ -56,18 +56,18 @@ def tile_picked_laythreecube_none_po_kernel(
         nc.gpsimd.memset(x_s[:, T // 2 :].bitcast(I32), 0)
         nc.gpsimd.memset(ws_raw[0][:].bitcast(I32), 0)
 
-        def load_scales(queues, tile, rows):
+        def load_scales(tile, rows):
             for q in range(QUADRANTS):
-                queues[q].dma_start(
+                nc.sync.dma_start(
                     tile[32 * q : 32 * q + PACK, :].bitcast(I32), rows[0, PACK * q : PACK * (q + 1), :].bitcast(I32)
                 )
 
         nc.sync.dma_start(lists["offs"][:], offs)
-        nc.scalar.dma_start(w_raw[0][:].bitcast(I32), w1_words[0].bitcast(I32))
         nc.scalar.dma_start(x_w[:].bitcast(I32), x_words[0].rearrange("p n t -> p (n t)").bitcast(I32))
-        load_scales([nc.sync] * QUADRANTS, x_s, x_scales)
-        load_scales([nc.sync] * (QUADRANTS - 1) + [nc.gpsimd], ws_raw[0], w1_scales)
-        nc.gpsimd.dma_start(gain[:], gn.rearrange("(p t) o -> p (t o)", t=PACK))
+        nc.sync.dma_start(w_raw[0][:].bitcast(I32), w1_words[0].bitcast(I32))
+        load_scales(x_s, x_scales)
+        load_scales(ws_raw[0], w1_scales)
+        nc.sync.dma_start(gain[:], gn.rearrange("(p t) o -> p (t o)", t=PACK))
 
         win1 = [sb("win1_%d" % t, [P, 2 * S], F32) for t in range(PACK)]
         win2 = [sb("win2_%d" % t, [P, 2 * S], F32) for t in range(PACK)]
@@ -82,7 +82,7 @@ def tile_picked_laythreecube_none_po_kernel(
 
         nc.sync.dma_start(lists["n1"][:], n1)
         nc.sync.dma_start(w_raw[1][:].bitcast(I32), w2_words[0].bitcast(I32))
-        load_scales([nc.sync] * QUADRANTS, ws_raw[1], w2_scales)
+        load_scales(ws_raw[1], w2_scales)
         nc.sync.dma_start(lists["n2"][:], n2)
         nc.sync.dma_start(lists["n3"][:], n3)
         nc.sync.dma_start(lists["n5"][:], n5)
@@ -121,9 +121,9 @@ def tile_picked_laythreecube_none_po_kernel(
         nc.vector.tensor_copy(picked_s[:], x_s[:].indirect(lists["offs"][:]))
         picked_lo = sb("picked_lo", [P, HALF], U32)
         nc.vector.tensor_copy(picked_lo[:], x_w[:].indirect(entries("offs", 0, HALF)))
-        deal_scales(0)
-        picked_hi = sb("picked_hi", [P, HALF], U32, tag="ws_raw0")
+        picked_hi = sb("picked_hi", [P, HALF], U32)
         nc.vector.tensor_copy(picked_hi[:], x_w[:].indirect(entries("offs", HALF, S)))
+        deal_scales(0)
         deal_words(1, tag="x_w")
         deal_scales(1)
         nc.scalar.mul(half_gain[:], gain[:], 0.5)

from contextlib import ExitStack

import concourse.mybir as mybir

K, T, S, N, H = 512, 2048, 512, 512, 512
P = 128
PACK = 4
QUADRANTS = 4
LIST_ROWS = 16
HALF = S // 2
FLOPS = 2 * K * H * S + 2 * H * N * S

F32 = mybir.dt.float32
BF16 = mybir.dt.bfloat16
I32 = mybir.dt.int32
U32 = mybir.dt.uint32
U16 = mybir.dt.uint16
U8 = mybir.dt.uint8
FP8X4 = mybir.dt.float8_e4m3fn_x4
FP4X4 = mybir.dt.float4_e2m1fn_x4
ALU = mybir.AluOpType
ACT = mybir.ActivationFunctionType

CHUNKS = ((0, 256), (256, 384), (384, 512))
LAST = len(CHUNKS) - 1


def interleave(copy, grouped, planes):
    copy(grouped.rearrange("p (c i t) -> p c t i", i=4, t=PACK), planes.rearrange("p t (c i) -> p c t i", i=4))


def tile_picked_laythreecube_none_po_kernel(
    tc, x_words, x_scales, w1_words, w1_scales, gn, w2_words, w2_scales, offs, n1, n2, n3, n4, n5, out_0, out_1, out_2
):
    nc = tc.nc
    with ExitStack() as ctx:
        keep = ctx.enter_context(tc.tile_pool(name="keep", bufs=1))
        psum = ctx.enter_context(tc.psum_pool(name="psum", bufs=1))

        def sb(name, shape, dtype, tag=None):
            return keep.tile(shape, dtype, name=name, tag=tag or name, align_bytes=64)

        lists = {name: sb("list_" + name, [P, S // LIST_ROWS], U16) for name in ("offs", "n1", "n2", "n3", "n4", "n5")}

        def entries(name, a, b):
            return lists[name][:, a // LIST_ROWS : b // LIST_ROWS]

        x_w = sb("x_w", [P, T], U32)
        x_s = sb("x_s", [P, T], U8)
        w_raw = [sb("w_raw%d" % layer, [P, 2 * H], U8) for layer in range(2)]
        ws_raw = [sb("ws_raw%d" % layer, [P, H], U8) for layer in range(2)]
        gain = sb("gain", [P, PACK], F32)
        half_gain = sb("half_gain", [P, PACK], F32)

        nc.vector.memset(x_s[:, : T // 2].bitcast(I32), 0)
        nc.gpsimd.memset(x_s[:, T // 2 :].bitcast(I32), 0)
        nc.gpsimd.memset(ws_raw[0][:].bitcast(I32), 0)

        def load_scales(tile, rows):
            for q in range(QUADRANTS):
                nc.sync.dma_start(
                    tile[32 * q : 32 * q + PACK, :].bitcast(I32), rows[0, PACK * q : PACK * (q + 1), :].bitcast(I32)
                )

        nc.sync.dma_start(lists["offs"][:], offs)
        nc.scalar.dma_start(x_w[:].bitcast(I32), x_words[0].rearrange("p n t -> p (n t)").bitcast(I32))
        nc.sync.dma_start(w_raw[0][:].bitcast(I32), w1_words[0].bitcast(I32))
        load_scales(x_s, x_scales)
        load_scales(ws_raw[0], w1_scales)
        nc.sync.dma_start(gain[:], gn.rearrange("(p t) o -> p (t o)", t=PACK))

        win1 = [sb("win1_%d" % t, [P, 2 * S], F32) for t in range(PACK)]
        win2 = [sb("win2_%d" % t, [P, 2 * S], F32) for t in range(PACK)]
        win5 = [
            sb("win5_%d" % t, [P, 2 * S], F32, tag="out_planes" if t == PACK - 2 else None) for t in range(PACK)
        ]
        nc.vector.memset(win1[0][:, S:], 0.0)
        nc.vector.memset(ws_raw[1][:].bitcast(I32), 0)
        for t in range(1, PACK):
            nc.scalar.copy(win1[t][:, S:], win1[0][:, S:])
        y = [win2[(t - 1) % PACK][:, S:] for t in range(PACK)]

        nc.sync.dma_start(lists["n1"][:], n1)
        nc.sync.dma_start(w_raw[1][:].bitcast(I32), w2_words[0].bitcast(I32))
        load_scales(ws_raw[1], w2_scales)
        nc.sync.dma_start(lists["n2"][:], n2)
        nc.sync.dma_start(lists["n3"][:], n3)
        nc.sync.dma_start(lists["n5"][:], n5)
        nc.sync.dma_start(lists["n4"][:], n4)

        w_dealt = {}
        ws_dealt = {}

        def deal_words(layer, tag=None):
            w_dealt[layer] = sb("w_dealt%d" % layer, [P, 2 * H], U8, tag=tag)
            nc.vector.tensor_copy(
                w_dealt[layer][:].rearrange("p (t m b) -> p t m b", t=PACK, b=2),
                w_raw[layer][:].rearrange("p (m t b) -> p t m b", t=PACK, b=2),
            )

        def deal_scales(layer):
            ws_dealt[layer] = sb("ws_dealt%d" % layer, [P, H], U8)
            nc.vector.tensor_copy(
                ws_dealt[layer][:].rearrange("p (t m) -> p t m", t=PACK),
                ws_raw[layer][:].rearrange("p (m t) -> p t m", t=PACK),
            )

        def product(layer, t, result, codes, scales):
            nc.tensor.matmul_mx(
                result,
                lhsT=w_dealt[layer][:, 2 * P * t : 2 * P * (t + 1)].bitcast(FP4X4),
                lhsT_scale=ws_dealt[layer][:, P * t : P * (t + 1)],
                rhs=codes.bitcast(FP8X4),
                rhs_scale=scales,
                start=True,
                stop=True,
            )

        picked_s = sb("picked_s", [P, S], U8)
        deal_words(0)
        nc.vector.tensor_copy(picked_s[:], x_s[:].indirect(lists["offs"][:]))
        picked_lo = sb("picked_lo", [P, HALF], U32)
        nc.vector.tensor_copy(picked_lo[:], x_w[:].indirect(entries("offs", 0, HALF)))
        picked_hi = sb("picked_hi", [P, HALF], U32)
        nc.vector.tensor_copy(picked_hi[:], x_w[:].indirect(entries("offs", HALF, S)))
        deal_scales(0)
        deal_words(1, tag="x_w")
        deal_scales(1)
        nc.scalar.mul(half_gain[:], gain[:], 0.5)
        picked = ((picked_lo, slice(0, HALF)), (picked_hi, slice(HALF, S)))

        for u, (words, cols) in enumerate(picked):
            bank = psum.tile([P, S], F32, name="plane0_%d" % u)
            product(0, 0, bank[:, :HALF], words[:], picked_s[:, cols])
            nc.scalar.mul(win1[0][:, cols], bank[:, :HALF], -1.0)
            nc.scalar.copy(y[0][:, cols], bank[:, :HALF])
        for t in range(1, PACK):
            bank = psum.tile([P, S], F32, name="plane%d" % t)
            for words, cols in reversed(picked):
                product(0, t, bank[:, cols], words[:], picked_s[:, cols])
            nc.scalar.mul(win1[t][:, :S], bank[:], -1.0)
            nc.scalar.copy(y[t], bank[:])

        h_tanh = [sb("h_tanh%d" % t, [P, S], F32) for t in range(PACK)]
        st_n2 = [sb("st_n2_%d" % t, [P, S], F32) for t in range(PACK)]
        su_own = [sb("su%d" % t, [P, S], F32) for t in range(PACK - 2, PACK)]
        su = [win1[t + 2][:, :S] for t in range(PACK - 2)] + [tile[:] for tile in su_own]
        gain_su = [win5[t][:, S:] for t in range(PACK)]
        win3 = [sb("win3_%d" % t, [P, S], F32) for t in range(PACK)]

        for step in range(PACK + 2):
            t = step
            if t < PACK:
                nc.vector.tensor_tensor(win2[t][:, :S], win1[t][:].indirect(lists["n1"][:]), y[t], ALU.add)
            t = step - 1
            if 0 <= t < PACK:
                nc.vector.tensor_copy(st_n2[t][:], win2[t][:].indirect(lists["n2"][:]))
            t = step - 2
            if 0 <= t:
                nc.vector.tensor_tensor(su[t], win2[t][:, :S], st_n2[t][:], ALU.max)
                nc.scalar.activation(win3[t][:], su[t], ACT.Copy, scale=half_gain[:, t : t + 1])
                nc.scalar.activation(gain_su[t], su[t], ACT.Copy, scale=gain[:, t : t + 1])

        h = [sb("h%d" % t, [P, S], F32) for t in range(PACK)]
        z_planes = {}
        z_tags = ("st_n2_2", "su3", "z_grouped0")

        def z_gather(c):
            a, b = CHUNKS[c]
            z_planes[c] = sb("z_planes%d" % c, [P, PACK, b - a], F32, tag=z_tags[c])
            for t in range(PACK):
                nc.vector.tensor_tensor(
                    z_planes[c][:, t, :], win3[t][:].indirect(entries("n3", a, b)), gain_su[t][:, a:b], ALU.add
                )

        def h_out(t, a, b, result):
            nc.scalar.activation(win5[t][:, a:b], result, ACT.Tanh)
            nc.scalar.copy(h[t][:, a:b], result)

        def z_product(c):
            a, b = CHUNKS[c]
            width = b - a
            grouped = sb("z_grouped%d" % c, [P, PACK * width], BF16)
            interleave(nc.vector.tensor_copy if c == LAST else nc.scalar.copy, grouped[:], z_planes[c][:])
            codes = sb("z_codes%d" % c, [P, width], U32)
            scales = sb("z_scales%d" % c, [P, width], U8)
            nc.vector.quantize_mx(codes[:].bitcast(FP8X4), scales[:], grouped[:])
            bank = psum.tile([P, S], F32, name="plane0_%d" % c)
            product(1, 0, bank[:, :width], codes[:], scales[:])
            if c == 0:
                product(1, PACK - 1, bank[:, width:], codes[:], scales[:])
                h_out(0, a, b, bank[:, :width])
                for t in range(1, PACK - 1):
                    early = psum.tile([P, S], F32, name="early%d" % t)
                    product(1, t, early[:, :width], codes[:], scales[:])
                    h_out(t, a, b, early[:, :width])
                h_out(PACK - 1, a, b, bank[:, width:])
            else:
                h_out(0, a, b, bank[:, :width])
                for t in range(1, PACK):
                    product(1, t, h_rest[t][:, a:b], codes[:], scales[:])

        h_rest = {t: psum.tile([P, S], F32, name="plane%d" % t) for t in range(1, PACK)}
        for c in range(len(CHUNKS)):
            z_gather(c)
            if c >= 1:
                z_product(c - 1)
        z_product(LAST)
        rest = CHUNKS[1][0]
        for t in range(1, PACK):
            h_out(t, rest, S, h_rest[t][:, rest:])

        for a, b in ((0, HALF), (HALF, S)):
            nc.vector.tensor_tensor(h_tanh[0][:, a:b], win5[0][:].indirect(entries("n5", a, b)), h[0][:, a:b], ALU.mult)
        for t in range(1, PACK):
            nc.vector.tensor_tensor(h_tanh[t][:], win5[t][:].indirect(lists["n5"][:]), h[t][:], ALU.mult)

        out_all = sb("out_all", [P, PACK * S], F32, tag="out_planes")
        out_planes = [out_all[:, PACK * a : PACK * b].rearrange("p (t c) -> p t c", t=PACK) for a, b in CHUNKS]
        out_scales = sb("out_scales", [P, S], U8)
        out_rows = out_0.rearrange("(p t) j -> p t j", t=PACK)
        out_words = out_1[0].rearrange("p n t -> p (n t)").bitcast(I32)
        out_grouped = [sb("out_grouped%d" % c, [P, PACK * (b - a)], BF16) for c, (a, b) in enumerate(CHUNKS)]

        def out_quantize(c):
            a, b = CHUNKS[c]
            codes = sb("out_codes%d" % c, [P, b - a], U32)
            nc.vector.quantize_mx(codes[:].bitcast(FP8X4), out_scales[:, a:b], out_grouped[c][:])
            nc.sync.dma_start(out_words[:, a:b], codes[:].bitcast(I32))

        for c, (a, b) in enumerate(CHUNKS):
            for t in range(PACK):
                nc.vector.tensor_tensor(
                    out_planes[c][:, t, :], h[t][:].indirect(entries("n4", a, b)), h_tanh[t][:, a:b], ALU.mult
                )
            nc.sync.dma_start(out_rows[:, :, a:b], out_planes[c])
            if c < LAST:
                interleave(nc.scalar.copy, out_grouped[c][:], out_planes[c])
        out_quantize(0)
        interleave(nc.vector.tensor_copy, out_grouped[LAST][:], out_planes[LAST])
        for c in range(1, len(CHUNKS)):
            out_quantize(c)
        for q in range(QUADRANTS):
            queue = nc.scalar if q % 2 == 0 else nc.sync
            queue.dma_start(
                out_2[0, PACK * q : PACK * (q + 1), :].bitcast(I32), out_scales[32 * q : 32 * q + PACK, :].bitcast(I32)
            )
